import numpy as np, ml_dtypes
CORES = [23,119,17,113]
N = 4
BF = ml_dtypes.bfloat16
def gentries(a):
    return np.ascontiguousarray(a.reshape(8, 16, -1).transpose(0, 2, 1)).reshape(8, -1)
def gtable(e):
    e = np.asarray(e); return np.ascontiguousarray(e.reshape(8, -1, 16).transpose(0, 2, 1)).reshape(128, -1).astype(np.int32)
W, V, I, RO = 4096, 2048, 256, 4
P = V // I
def parts(rng):
    return (rng.integers(0, W, (N, 8, 16, W)), rng.integers(0, 256, (N, 8, 16, V)), rng.integers(0, 256, (N, 8, 16, I)),
            rng.integers(0, W, (N, 8, I)), rng.integers(0, 256, (N, 8, 16)))
def pack(S, X, x, s, w):
    return {"stm": np.ascontiguousarray(S.reshape(N, 128, W)).astype(np.int32), "vx": X.reshape(N, 128, V).astype(np.float32).astype(BF),
            "x0": x.reshape(N, 128, I).astype(np.float32).astype(BF), "s0": np.stack([gtable(a) for a in s]), "wt": w.reshape(N, 128, 1).astype(np.int32)}
def two(rng, lo, hi, shape):
    return np.where(rng.random(shape) < 0.5, lo, hi)
def tame(rng, S, w, cl):
    col = np.arange(W); ev = col[((col >> 4) & 1) == 0]
    off = np.where(cl, 0, rng.integers(1, 16, cl.shape))
    S[:, ev] = 32 * np.argsort(rng.random((16, W // 32, 16)), axis=1).reshape(16, W // 2) + 16 + ((ev + off) & 15)
    w[:] = 32 * rng.integers(1, 8, 16)
    return ev
def lay(rng, S, w, cl, no):
    off = rng.integers(1, 15, cl.shape); off = np.where(cl, 0, off + (off >= 16 - no))
    S[:] = 16 * rng.integers(0, W // 16, cl.shape) + ((np.arange(W) + off) & 15)
    w[:] = 32 * rng.integers(1, 8, 16)
def wake(S, X, w, k, c):
    if (S[k, c] & (V - 1)) == (S[k ^ 1, c] & (V - 1)): S[k ^ 1, c] = S[k ^ 1, c] ^ 16
    a = S[k, c] & (V - 1); b = S[k ^ 1, c] & (V - 1)
    X[0, b] = X[0, a] ^ 1
    if int(np.add.reduce(w * np.abs(X[:, a] - X[:, b]))) & (W - 1) == 0: w[0] = w[0] ^ 32
def setup_inputs(rng):
    return pack(*parts(rng))
def setup_inputs_corners(rng):
    S, X, x, s, w = parts(rng); M = W // 2; role = rng.permutation(N)
    for q in range(N):
        kinds = rng.permutation(8); gx = int(rng.integers(0, 8))
        for g in range(8):
            kind = int(kinds[g])
            if role[q] == 0 or role[q] == 2: kind = 0 if g % 2 == 0 else 2
            if role[q] == 1: kind = 1
            if role[q] == 2 and g == gx: kind = 8
            if kind == 6:
                S[q, g] = np.arange(W)[None, :]; s[q, g, 0] = W - 1; s[q, g, I - 1] = 0; continue
            if kind == 7:
                s[q, g] = two(rng, 0, W - 1, I); continue
            cl = np.zeros((16, M), bool); p = rng.permutation(M)
            if kind == 1: cl[:] = True
            if kind == 2: cl[15] = True
            if kind == 3: cl[0] = True; cl[15] = True
            if kind == 4: cl[14:] = rng.random(M) < 0.5
            if kind == 5: cl = np.argsort(rng.random((16, M)), axis=0) < rng.integers(0, 17, M)
            if kind == 8:
                n = int(rng.integers(15, 18)); cl[3, p[:n]] = True; cl[9, p[:n]] = True
            ev = tame(rng, S[q, g], w[q, g], cl)
            s[q, g] = rng.permutation(ev[p[:I]])
    return pack(S, X, x, s, w)
def setup_inputs_late(rng):
    S, X, x, s, w = parts(rng); odd = int(rng.integers(0, 2)); col = np.arange(W)
    for q in range(N):
        if q % 2 == odd:
            al = int(rng.integers(1, 16)); n = 16 * int(rng.integers(I // 16, 5 * I // 16)) + al
            fk = rng.permutation(8 * (I - 1)).reshape(8, I - 1) < n
            for g in range(8):
                m = np.where((col & 1) == 1, rng.integers(0, 2, W), rng.integers(2, 5, W)); m[W - 1] = 0
                lay(rng, S[q, g], w[q, g], np.argsort(rng.random((16, W)), axis=0) < m, al)
                s[q, g] = 2 * rng.integers(0, W // 2, I) + 1; s[q, g, :I - 1] -= fk[g].astype(np.int64); s[q, g, I - 1] = W - 1
            continue
        kinds = rng.permutation(8)
        for g in range(8):
            kind = int(kinds[g]) // 2; Sg, Xg, wg = S[q, g], X[q, g], w[q, g]
            if kind == 3: continue
            no = int(rng.integers(1, 16)); e = 16 * (1 + rng.permutation(W // 16 - 1)[:4])
            if kind == 0:
                lay(rng, Sg, wg, np.zeros((16, W), bool), no)
                k = int(rng.integers(0, 16)); c = int(rng.integers(0, W)); at = np.arange(c & 15, W, 16)
                Sg[k, at] = c; s[q, g] = rng.choice(at, I); wake(Sg, Xg, wg, k, c); continue
            lay(rng, Sg, wg, rng.random((16, W)) < 0.0625, no)
            if kind == 1:
                Sg[Sg == 0] = 16
                Sg[0, e[0]] = 0; Sg[0, e[1]] = 5; Sg[1, e[1]] = 0
                s[q, g, 0] = e[0]; s[q, g, 1] = e[1]; wake(Sg, Xg, wg, 0, 0)
            if kind == 2:
                ka = int(rng.integers(0, 15)); kb = int(rng.integers(ka + 1, 16))
                Sg[:, e] = 16 * rng.integers(0, W // 16, (16, 4)) + rng.integers(1, 16, (16, 4))
                Sg[ka, e] = 16 * rng.integers(1, W // 16, 4); Sg[kb, e] = 0
                z = np.abs(Xg[:, Sg[kb, 0] & (V - 1)] - Xg[:, Sg[kb ^ 1, 0] & (V - 1)])
                s[q, g, 1::2] = rng.choice(e, I // 2); x[q, g, :, 1::2] = z[:, None]
    return pack(S, X, x, s, w)
def setup_inputs_ties(rng):
    S, X, x, s, w = parts(rng)
    pool = np.argsort(rng.random((N, 8, W)), axis=-1)[..., :32]; pool[..., 0] = W - 1; pool[..., 1] = 0
    S = np.take_along_axis(pool[:, :, None, :], rng.integers(0, 32, (N, 8, 16, W)), 3)
    s = np.take_along_axis(pool, rng.integers(0, 32, (N, 8, I)), 2)
    few = np.take_along_axis(X[..., :5], rng.integers(0, 5, (N, 8, 1, V)), 3)
    X[:, ::2] = few[:, ::2]; x[:, 1::2] = x[:, 1::2, :, :1]
    return pack(S, X, x, s, w)
def setup_inputs_ends(rng):
    S, X, x, s, w = parts(rng)
    S = np.where(rng.random(S.shape) < 0.7, two(rng, 0, W - 1, S.shape), S)
    S[..., 0] = two(rng, 0, W - 1, (N, 8, 16)); S[..., W - 1] = two(rng, 0, W - 1, (N, 8, 16))
    S[:, :, [0, 1, 14, 15], 0] = np.array([0, W - 1, 0, W - 1]); S[:, :, [0, 1, 14, 15], W - 1] = np.array([0, W - 1, W - 1, 0])
    S[:, :, 4:6, 0] = 0; S[:, :, 4:6, W - 1] = W - 1
    q = 16 * rng.integers(1, W // 16 - 1, (N, 8)); S[:, :, 2, 0] = q; S[:, :, 2, W - 1] = q + 15
    for a in range(N):
        for g in range(8):
            S[a, g, 2:4, q[a, g]] = W - 1; S[a, g, 2:4, q[a, g] + 15] = 0
    S[:, :, 1, W - 2] = W - 1; S[:, :, 15, W - 2] = W - 1
    X = two(rng, 0, 255, X.shape); X[..., 0] = 0; X[..., V - 1] = 255
    x = two(rng, 0, 255, x.shape); w = two(rng, 0, 255, w.shape)
    w[:, 0] = 255; w[:, 7] = 255; w[:, 1::5] = 0; w[:, 1::5, 15] = 255; w[:, 1::5, 14] = 2
    s = np.where(rng.random(s.shape) < 0.8, two(rng, 0, W - 1, s.shape), s); s[N - 1] = two(rng, 0, W - 1, (8, I))
    s[:, 7, I - 1] = W - 1; s[:, 0, 2] = W - 1; s[:, 7, 1] = 0
    s[:, 1::5, 3] = W - 2; s[:, 1::5, I - 1] = W - 2; s[:, 1::5, I - 2] = W - 1; s[:, 1::5, 4] = W - 1
    return pack(S, X, x, s, w)
def setup_inputs_spread(rng):
    S, X, x, s, w = parts(rng)
    p = rng.choice(np.array([1.0, 1.5, 2.0, 4.0]), (N, 8, 1, 1)); fl = rng.random((N, 8, 1, 1)) < 0.5
    S = np.minimum((W * rng.random(S.shape) ** p).astype(np.int64), W - 1); S = np.where(fl, W - 1 - S, S)
    s = np.minimum((W * rng.random(s.shape) ** p[..., 0]).astype(np.int64), W - 1)
    X = np.minimum((np.exp2(8 * rng.random((N, 8, 1, V))) * rng.random(X.shape)).astype(np.int64), 255)
    x = np.minimum((np.exp2(8 * rng.random((N, 8, 1, I))) * rng.random(x.shape)).astype(np.int64), 255)
    w = np.minimum(np.exp2(8 * rng.random(w.shape)).astype(np.int64), 255)
    return pack(S, X, x, s, w)
def check_inputs(d):
    bad = []
    for k, lo, hi in (("stm", 0, W - 1), ("vx", 0, 255), ("x0", 0, 255), ("s0", 0, W - 1), ("wt", 0, 255)):
        v = np.asarray(d[k]).astype(np.float64)
        if not (np.min(v) >= lo and np.max(v) <= hi): bad.append("range of " + k)
        elif np.any(v != np.floor(v)): bad.append("whole numbers in " + k)
    return bad
def reference(stm, vx, x0, s0, wt):
    S = stm.astype(np.int64).reshape(N, 8, 16, W); X = vx.astype(np.float32).astype(np.int64).reshape(N, 8, 16, V)
    x = x0.astype(np.float32).astype(np.int64).reshape(N, 8, 16, I); w = wt.astype(np.int64).reshape(N, 8, 16, 1, 1)
    s = np.stack([gentries(a) for a in s0]).astype(np.int64)
    A = np.zeros(N, np.int64); mate = np.arange(16) ^ 1
    for t in range(RO):
        c = np.take_along_axis(S, s[:, :, None, :], 3)
        a = np.take_along_axis(S, c, 3) & (V - 1); b = np.take_along_axis(S[:, :, mate], c, 3) & (V - 1)
        z = np.abs(np.take_along_axis(X, a.reshape(N, 8, 1, 16 * I), 3) - np.take_along_axis(X, b.reshape(N, 8, 1, 16 * I), 3)).reshape(N, 8, 16, 16, I)
        u = np.add.reduce(w * z, axis=2) & (W - 1)
        claim = ((((u * u) >> 5) + u + c + A[:, None, None, None]) & 15) == (s & 15)[:, :, None, :]
        n = np.add.accumulate(claim.astype(np.int64), axis=2)
        has = n[:, :, 15] >= 1; fork = n[:, :, 15] >= 2
        k1 = np.argmax(claim & (n == 1), axis=2); k2 = np.argmax(claim & (n == 2), axis=2)
        c1 = np.take_along_axis(c, k1[:, :, None, :], 2)[:, :, 0]; c2 = np.take_along_axis(c, k2[:, :, None, :], 2)[:, :, 0]
        u1 = np.take_along_axis(u, k1[:, :, None, :], 2)[:, :, 0]
        z1 = np.take_along_axis(z, k1[:, :, None, None, :], 3)[:, :, :, 0]; z2 = np.take_along_axis(z, k2[:, :, None, None, :], 3)[:, :, :, 0]
        h = 1 + t % (N - 1)
        came = np.roll(fork, h, axis=0); cc = np.roll(c2, h, axis=0); cx = np.roll(np.abs(x - z2), h, axis=0)
        s = np.where(has, c1, np.where(came, cc, (5 * s + u[:, :, 0]) & (W - 1)))
        x = np.where(has[:, :, None], (x + z1) >> 1, np.where(came[:, :, None], cx, x))
        for r in range(N):
            for g in range(8):
                i = np.flatnonzero(has[r, g])
                X[r, g][:, P * i + (u1[r, g, i] & (P - 1))] = z1[r, g][:, i]
                col, at = np.unique(c1[r, g, i], return_index=True)
                i = i[at]; k = k1[r, g, i]
                S[r, g, k, col] = (S[r, g, k, col] + u1[r, g, i]) & (W - 1)
        A = np.add.reduce(fork.astype(np.int64), axis=(1, 2)) & 15
    return {"yt": np.add.reduce(S.reshape(N, 128, W // 256, 256), axis=2).astype(np.float32), "yv": X.reshape(N, 128, V).astype(np.float32).astype(BF),
            "yx": x.reshape(N, 128, I).astype(np.float32).astype(BF), "ys": np.stack([gtable(e) for e in s]).astype(np.float32)}

from concourse.mybir import AluOpType as A, ActivationFunctionType as F

STEPS = 4
NCH = 4
CW = 64
GRP = ((0, 192), (192, 256))
OFF = (0, 256, 768, 1536)
MAGIC = 12582912.0
SG_SCALAR = (1, 3)
Y_TENSOR = (0,)
LOADS = (0, 1536, 2816, 3712, 4096)
XR, XD = 2560, 4608
XCY, XCH = 256, 640

PF = {}
for _i, _nm in enumerate(("hm", "cand", "kb", "hm2", "m0", "nw", "ndv", "pm", "w1", "w2", "cm", "xm", "xi", "s5",
                          "Ic", "I16", "I32", "KC", "Dc", "r16", "q16", "cM")):
    PF[_nm] = ("lf", 16 * _i)
for _i, _nm in enumerate(("sm", "n0i", "n0", "m1", "yi", "y7", "sL1", "sL2", "sL3", "sL4")):
    PF[_nm] = ("li", 16 * _i)
for _i, _nm in enumerate(("c1U", "posU", "WLU", "XLU", "sU0", "sU1", "sU2", "sU3")):
    PF[_nm] = ("lu", 16 * _i)
for _i, _nm in enumerate(("ui", "um", "tt", "tb", "nc", "nd")):
    PF[_nm] = ("gi", 256 * _i)
for _i, _nm in enumerate(("sq", "FU", "ha", "ki", "yto", "qn")):
    PF[_nm] = ("gf", 256 * _i)

SCRATCH = {
    "lf": ("sbuf", [128, 22 * 16], "float32"),
    "li": ("sbuf", [128, 10 * 16], "int32"),
    "lu": ("sbuf", [128, 8 * 16], "uint16"),
    "gi": ("sbuf", [128, 6 * 256], "int32"),
    "gf": ("sbuf", [128, 6 * 256], "float32"),
    "smA": ("sbuf", [128, 16], "float16"),
    "sL0": ("sbuf", [128, 16], "int32"),
    "Si": ("sbuf", [128, 4096], "int32"),
    "Sw": ("sbuf", [128, 4352], "float32"),
    "XX": ("sbuf", [128, 6656], "bfloat16"),
    "on": ("sbuf", [128, 2048], "bfloat16"),
    "DA": ("sbuf", [128, 16, 8, 16], "bfloat16"),
    "DB": ("sbuf", [128, 16, 8, 16], "bfloat16"),
    "LR": ("sbuf", [128, 16, 8, 16], "bfloat16"),
    "WU": ("sbuf", [128, 16, 8, 16], "bfloat16"),
    "ER": ("sbuf", [128, 16, 128], "bfloat16"),
    "BG": ("sbuf", [128, 8], "bfloat16"),
    "BH": ("sbuf", [128, 8], "bfloat16"),
    "BI": ("sbuf", [128, 128], "bfloat16"),
    "BM": ("sbuf", [128, 128], "bfloat16"),
    "BM10": ("sbuf", [128, 128], "bfloat16"),
    "BM8": ("sbuf", [128, 128], "bfloat16"),
    "Id": ("sbuf", [128, 8, 16], "bfloat16"),
    "IdN": ("sbuf", [128, 128], "bfloat16"),
    "Id32": ("sbuf", [128, 128], "bfloat16"),
    "IdM": ("sbuf", [128, 8, 16], "bfloat16"),
    "CNT": ("sbuf", [128, 8, 16], "bfloat16"),
    "CN2": ("sbuf", [128, 8, 16], "bfloat16"),
    "half": ("sbuf", [128, 128], "float32"),
    "mhalf": ("sbuf", [128, 256], "bfloat16"),
    "RS": ("sbuf", [128, 2560], "bfloat16"),
    "kr5": ("sbuf", [128, 256], "bfloat16"),
    "pI": ("sbuf", [128, 1], "int32"),
    "pJ": ("sbuf", [128, 1], "int32"),
    "kcol": ("sbuf", [128, 1], "float32"),
    "row0": ("sbuf", [128, 1], "float32"),
    "c16": ("sbuf", [128, 1], "float32"),
    "Jc": ("sbuf", [128, 2, 16], "bfloat16"),
    "wI": ("sbuf", [128, 1], "int32"),
    "wF": ("sbuf", [128, 1], "float32"),
    "AD": ("sbuf", [128, 2560], "bfloat16"),
    "SC": ("sbuf", [128, 2560], "bfloat16"),
    "jk": ("sbuf", [128, 16], "bfloat16"),
    "acc": ("sbuf", [128, 1], "float32"),
    "S16": ("sbuf", [128, 4096], "float16"),
    "yso": ("sbuf", [128, 16], "float32"),
    "AB": ("sbuf", [128, 512], "uint16"),
    "G": ("sbuf", [128, 4096], "float16"),
    "Xa": ("sbuf", [128, 4096], "bfloat16"),
    "WN": ("sbuf", [128, 16, 8, 16], "bfloat16"),
    "W2": ("sbuf", [128, 16, 8, 16], "bfloat16"),
    "yF": ("sbuf", [128, 256], "float16"),
    "Fp": ("sbuf", [128, 256], "float16"),
    "z2": ("sbuf", [128, 256], "bfloat16"),
    "ab0": ("psum", [128, 512], "float32"),
    "ab1": ("psum", [128, 512], "float32"),
    "us0": ("psum", [128, 512], "float32"),
    "us1": ("psum", [128, 512], "float32"),
    "ec": ("psum", [128, 512], "float32"),
    "qc": ("psum", [128, 512], "float32"),
    "kr": ("psum", [128, 512], "float32"),
    "L": ("psum", [128, 32, 16], "float32"),
}
for _t in range(STEPS):
    SCRATCH["snd%d" % _t] = ("sbuf", [128, 16], "float32")
    SCRATCH["rcv%d" % _t] = ("sbuf", [128, 16], "float32")
    SCRATCH["Y%d" % _t] = ("sbuf", [128, 256], "bfloat16")
for _t in range(STEPS + 1):
    SCRATCH["XC%d" % _t] = ("sbuf", [128, 896], "bfloat16")
for _p in range(2):
    SCRATCH["D%d" % _p] = ("sbuf", [128, 4096], "bfloat16")
    SCRATCH["Z%d" % _p] = ("sbuf", [128, 4096], "bfloat16")
    SCRATCH["z1%d" % _p] = ("sbuf", [128, 256], "bfloat16")
    SCRATCH["cU%d" % _p] = ("sbuf", [128, 256], "uint16")
    SCRATCH["cF%d" % _p] = ("sbuf", [128, 256], "float16")
for _g, (_a, _b) in enumerate(GRP):
    _n = _b - _a
    SCRATCH["Fb%d" % _g] = ("sbuf", [128, 2, _n], "float16")
    SCRATCH["Qt%d" % _g] = ("sbuf", [128, 7, _n], "float16")
    SCRATCH["JU%d" % _g] = ("sbuf", [128, 2, _n // 16], "uint16")

SEMAPHORES = ["eV", "eS", "eP", "eG"] + ["m%d" % i for i in range(24)]
for _t in range(STEPS):
    SEMAPHORES += ["an%d" % _t, "ax%d" % _t, "ln%d" % _t, "lx%d" % _t]

EST = {"cyc": 0.00083 * 1.2, "fix": 0.05, "ga": 1.55, "sc": 3.8, "pe": 0.00075 * 1.15, "wake": 0.12, "net": 3.0}
BOOST = {}
LOOK = 0.001
RELU_V = (2, 3)
PSUMS = ("ab0", "ab1", "us0", "us1", "ec", "qc", "kr", "L")
WIDTH = {}
for _k in SCRATCH:
    _w = 1
    for _d in SCRATCH[_k][1][1:]:
        _w *= _d
    WIDTH[_k] = _w


def rng(x):
    name, lo, hi = x if isinstance(x, tuple) else (x, None, None)
    if name in PF:
        b, o = PF[name]
        if lo is None:
            lo, hi = 0, (16 if b[0] == "l" else 256)
        return (b, o + lo, o + hi)
    if lo is None:
        lo, hi = 0, WIDTH[name]
    return (name, lo, hi)


def build(core, T, topo, ops):
    rank = T.rank_of(core)
    cyc, fix = EST["cyc"], EST["fix"]
    GA, SCT = EST["ga"], EST["sc"]

    cls = ["x"]

    def add(q, fn, dur, r, w, kind="c", sem=None, cnt=1):
        ops.append({"q": q, "fn": fn, "dur": dur, "r": [rng(x) for x in r], "w": [rng(x) for x in w], "kind": kind, "sem": sem, "cnt": cnt, "cls": cls[0]})

    def V(fn, n, r, w):
        add("V", fn, fix + cyc * max(64, n), r, w)

    def S(fn, n, r, w):
        add("S", fn, fix + 0.01 + cyc * max(64, n), r, w)

    def P(fn, n, r, w):
        add("P", fn, 0.03 + EST["pe"] * n, r, w)

    def G(fn, n, r, w):
        add("G", fn, 0.17 + 2 * cyc * n, r, w)

    ndma = [0]

    def dma(q, out, in_, dur, r, w):
        s = "m%d" % ndma[0]
        ndma[0] += 1
        add(q, lambda e: e.dma_start(out, in_), dur, r, w, "dma", s, 16)

    def pf(name, lo=None, hi=None):
        b, lo, hi = rng(name if lo is None else (name, lo, hi))
        return T[b][:, lo:hi]

    def ts(out, i0, s1, s2, op0, op1=None):
        if op1 is None:
            return lambda e: e.tensor_scalar(out, i0, s1, None, op0)
        return lambda e: e.tensor_scalar(out, i0, s1, s2, op0, op1)

    def tt(out, i0, i1, op):
        return lambda e: e.tensor_tensor(out, i0, i1, op)

    def cp(out, i0):
        return lambda e: e.tensor_copy(out, i0)

    def act(out, i0, f, **k):
        return lambda e: e.activation(out, i0, f, **k)

    def asel(out, i0, pat, op, base, cm):
        return lambda e: e.affine_select(out, i0, pat, op, 0.0, base, cm)

    def mms(calls):
        def run(e):
            last = None
            for c in calls:
                last = e.matmul(c[0], c[1], c[2], c[3], c[4])
            return last
        return run

    dma("Y", T.sL0[:], T.s0[:], 2.0, [], ["sL0"])
    for j in range(4):
        a, b = LOADS[j], LOADS[j + 1]
        dma("Y" if j % 2 == 0 else "S", T.Si[:, a:b], T.stm[:, a:b], 2.0 + (b * 7.0 / 4096), [], [("Si", a, b)])
    dma("Y", T.wI[:], T.wt[:], 6.0, [], ["wI"])
    dma("Y", T.XX[:, XR:XR + 2048], T.vx[:], 9.0, [], [("XX", XR, XR + 2048)])
    dma("Y", T.XX[:, XD:XD + 2048], T.vx[:], 10.0, [], [("XX", XD, XD + 2048)])
    dma("Y", T.XC0[:, 0:256], T.x0[:], 10.5, [], [("XC0", 0, 256)])

    V(lambda e: e.memset(T.on[:], 1.0), 1024, [], ["on"])
    G(asel(T.BH[:], T.on[:, 0:8], [[-16, 8]], A.is_ge, 0, 1), 8, ["on"], ["BH"])
    G(asel(T.BG[:], T.BH[:], [[16, 8]], A.is_ge, 15, -1), 8, ["BH"], ["BG"])
    G(asel(T.BI[:], T.on[:, 0:128], [[-16, 8], [0, 16]], A.is_ge, 0, 1), 128, ["on"], ["BI"])
    G(asel(T.BM[:], T.BI[:], [[16, 8], [0, 16]], A.is_ge, 15, -1), 128, ["BI"], ["BM"])
    G(lambda e: e.iota(T.pI[:], [[0, 1]], 0, 1), 1, [], ["pI"])
    G(lambda e: e.iota(pf("r16"), [[1, 16]], 0, 0, allow_small_or_imprecise_dtypes=True), 16, [], ["r16"])
    G(lambda e: e.iota(pf("q16"), [[16, 16]], 0, 0, allow_small_or_imprecise_dtypes=True), 16, [], ["q16"])
    G(asel(T.DA[:], T.on[:], [[1000, 16], [-16, 8], [-1001, 16]], A.is_equal, 0, 1), 2048, ["on"], ["DA"])
    G(asel(T.DB[:, 0::2, :, :], T.on[:, 0:1024], [[2000, 8], [-16, 8], [-1001, 16]], A.is_equal, -1, 1), 1024, ["on"], ["DB"])
    G(asel(T.DB[:, 1::2, :, :], T.on[:, 0:1024], [[2000, 8], [-16, 8], [-1001, 16]], A.is_equal, 1001, 1), 1024, ["on"], ["DB"])
    G(asel(T.CNT[:], T.BM[:], [[1, 128]], A.is_ge, -1, -1), 128, ["BM"], ["CNT"])
    G(asel(T.Id[:], T.on[:, 0:128], [[-1, 128]], A.is_equal, 0, 1), 128, ["on"], ["Id"])
    G(lambda e: e.iota(pf("ki"), [[1, 256]], -64, 0, allow_small_or_imprecise_dtypes=True), 256, [], ["ki"])
    V(lambda e: e.memset(T.LR[:], 0.0), 1024, [], ["LR"])
    V(ts(T.pJ[:], T.pI[:], 15, None, A.bitwise_and), 1, ["pI"], ["pJ"])
    V(cp(T.kcol[:], T.pJ[:]), 1, ["pJ"], ["kcol"])
    V(ts(pf("cM"), pf("r16"), T.kcol[:], -32.0, A.is_equal, A.mult), 16, ["r16", "kcol"], ["cM"])
    for r in range(16):
        S(act(T.LR[:, r, :, r], T.BG[:], F.Copy), 8, ["BG"], [("LR", 128 * r, 128 * r + 128)])
        S(act(T.ER[:, r, :], T.BM[:], F.Copy, scale=pf("cM", r, r + 1)), 128, ["BM", "cM"], [("ER", 128 * r, 128 * r + 128)])
    V(cp(T.wF[:], T.wI[:]), 1, ["wI"], ["wF"])
    V(ts(T.WU[:], T.LR[:], T.wF[:], None, A.mult), 1024, ["LR", "wF"], ["WU"])
    V(ts(T.WN[:], T.WU[:], -1.0, None, A.mult), 1024, ["WU"], ["WN"])
    V(ts(T.W2[:], T.WU[:], 2.0, None, A.mult), 1024, ["WU"], ["W2"])
    V(ts(pf("Ic"), pf("q16"), T.kcol[:], None, A.add), 16, ["q16", "kcol"], ["Ic"])
    for nm, f, a in (("I16", 16.0, 0.0), ("I32", 32.0, 0.0), ("KC", -1.0 / 512, 0.25), ("Dc", 1.0, 12288.0)):
        S(act(pf(nm), pf("Ic"), F.Identity, scale=f, bias=a), 16, ["Ic"], [nm])
    for h in range(2):
        S(act(T.Jc[:, h, :], pf("Ic"), F.Copy, scale=16.0), 16, ["Ic"], [("Jc", 16 * h, 16 * h + 16)])
    V(ts(T.IdM[:], T.Id[:], -100.0, None, A.mult), 64, ["Id"], ["IdM"])
    V(lambda e: e.memset(T.c16[:], 16.0), 1, [], ["c16"])
    for nm, f in (("Id32", 32.0), ("IdN", -1.0)):
        S(act(T[nm][:], T.Id[:], F.Copy, scale=f), 128, ["Id"], [nm])
    for nm, f in (("BM10", 10240.0), ("BM8", 0.125)):
        S(act(T[nm][:], T.BM[:], F.Copy, scale=f), 128, ["BM"], [nm])
    V(tt(T.CN2[:], T.CNT[:], T.IdM[:], A.add), 256, ["CNT", "IdM"], ["CN2"])
    S(act(T.kr5[:], pf("ki"), F.Copy, scale=1.0 / 512), 256, ["ki"], ["kr5"])
    V(ts(T.row0[:], T.kcol[:], 0.0, None, A.is_equal), 1, ["kcol"], ["row0"])
    V(lambda e: e.memset(T.RS[:], 0.0), 1280, [], ["RS"])
    for ch in range(NCH):
        o, w = OFF[ch], 64 * (ch + 1)
        V(lambda e, o=o, w=w: e.memset(T.RS[:, o:o + 4 * w:w], 1048576.0), 8, [], [("RS", o, o + 4 * w)])
    for t in range(STEPS):
        V(lambda e, t=t: e.memset(T["XC%d" % t][:, 512:XCH], 0.0), 64, [], [("XC%d" % t, 512, XCH)])
    V(lambda e: e.memset(T.half[:], 0.5), 128, [], ["half"])
    V(lambda e: e.memset(T.mhalf[:], -0.5), 128, [], ["mhalf"])
    V(cp(pf("sU0"), T.sL0[:]), 16, ["sL0"], ["sU0"])
    for j in range(4):
        a, b = LOADS[j], LOADS[j + 1]
        V(cp(T.Sw[:, a:b], T.Si[:, a:b]), b - a, [("Si", a, b)], [("Sw", a, b)])

    SW = ("Sw", 0, 4096)
    XW = ("XX", XR, XR + 4096)

    def step(t):
        p = t % 2
        n = str(t)
        sLn, sUn = "sL" + n, "sU" + n
        sL = T.sL0[:] if t == 0 else pf(sLn)
        cU, cF, Z, D, z1 = T["cU%d" % p], T["cF%d" % p], T["Z%d" % p], T["D%d" % p], T["z1%d" % p]
        cUn, cFn, Zn, Dn, z1n = "cU%d" % p, "cF%d" % p, "Z%d" % p, "D%d" % p, "z1%d" % p
        XC, XCn = T["XC" + n], "XC" + n
        swin = T.Sw[:, 0:4096]
        xwin = T.XX[:, XR:XR + 4096]
        for lo, hi in ((0, 64), (64, 256)):
            V(cp(cU[:, lo:hi], swin.indirect(pf(sUn, lo // 16, hi // 16))), GA * (hi - lo), [SW, sUn], [(cUn, lo, hi)])
        V(ts(pf("sm"), sL, 15, None, A.bitwise_and), 16, [sLn], ["sm"])
        V(ts(pf("s5"), sL, 5.0, None, A.mult), 16, [sLn], ["s5"])
        if t == 0:
            V(ts(T.smA[:], pf("sm"), 8.0, None, A.add), 16, ["sm"], ["smA"])
        else:
            V(ts(T.smA[:], pf("sm"), T.L[:, 8, 0:1], 8.0, A.subtract, A.add), 16, ["sm", ("L", 128, 129)], ["smA"])
        V(ts(cF[:], cU[:], -2048.0, None, A.add), 128, [cUn], [cFn])
        for ch in range(NCH):
            a, b = 1024 * ch, 1024 * ch + 1024
            w = swin.indirect(cU[:, CW * ch:CW * ch + CW])
            r, wr = [SW, (cUn, CW * ch, CW * ch + CW)], [("G", a, b)]
            if ch in SG_SCALAR:
                S(act(T.G[:, a:b], w, F.Identity, bias=-2048.0), GA * 1024, r, wr)
            else:
                V(ts(T.G[:, a:b], w, -2048.0, None, A.add), GA * 1024, r, wr)
        calls = [(T.ec[:, 0:256], T.Id32[:], cF[:], True, False)]
        for r in range(16):
            calls.append((T.ec[:, r:256:16], T.ER[:, r, :], T.smA[:], False, r == 15))
        calls.append((T.ec[:, 256:512], T.Id[:], cF[:], True, True))
        P(mms(calls), 512 + 1024, ["Id32", "Id", "ER", "smA", cFn], ["ec"])

        def chunk(ch):
            a, b = 1024 * ch, 1024 * ch + 1024
            abn = ("ab0", "ab1", "us1", "ab1")[ch]
            ao = 256 if abn == "us1" else 0
            ab = T[abn][:, ao:ao + 128]
            A0, A1, A2 = 128 * ch, 128 * ch + 64, 128 * ch + 128
            calls = []
            for o, M in ((0, T.DA), (CW, T.DB)):
                for k in range(16):
                    calls.append((ab[:, o:o + CW], M[:, k, :, :], T.G[:, a + k:b:16], k == 0, k == 15))
            P(mms(calls), 2048, ["DA", "DB", ("G", a, b)], [(abn, ao, ao + 128)])
            V(ts(T.AB[:, A0:A2], ab, 2048.0, None, A.add), 128, [(abn, ao, ao + 128)], [("AB", A0, A2)])
            S(act(T.Xa[:, a:b], xwin.indirect(T.AB[:, A0:A1]), F.Copy), GA * 1024, [XW, ("AB", A0, A1)], [("Xa", a, b)])
            V(tt(D[:, a:b], xwin.indirect(T.AB[:, A1:A2]), T.Xa[:, a:b], A.subtract), GA * 1024, [XW, ("AB", A1, A2), ("Xa", a, b)], [(Dn, a, b)])
            gi = [i for i in range(len(GRP)) if GRP[i][0] <= CW * ch < GRP[i][1]][0]
            un, o = "us%d" % gi, CW * ch - GRP[gi][0]
            uo = T[un][:, o:o + CW]
            if ch in RELU_V:
                V(ts(Z[:, a:b], D[:, a:b], 0.0, None, A.max), 512, [(Dn, a, b)], [(Zn, a, b)])
                wn = [(uo, T.WN[:, k, :, :], D[:, a + k:b:16], k == 0, False) for k in range(16)]
                w2 = [(uo, T.W2[:, k, :, :], Z[:, a + k:b:16], False, k == 15) for k in range(16)]
                if GRP[gi][1] - GRP[gi][0] == CW:
                    P(mms(wn), 1024, ["WN", (Dn, a, b), (un, 256, 384)], [(un, o, o + CW)])
                    P(mms(w2), 1024, ["W2", (Zn, a, b), (un, o, o + CW), (un, 256, 384)], [(un, o, o + CW)])
                else:
                    P(mms(wn + w2), 2048, ["WN", "W2", (Dn, a, b), (Zn, a, b)], [(un, o, o + CW)])
            else:
                S(act(Z[:, a:b], D[:, a:b], F.Abs), 1024, [(Dn, a, b)], [(Zn, a, b)])
                P(mms([(uo, T.WU[:, k, :, :], Z[:, a + k:b:16], k == 0, k == 15) for k in range(16)]), 1024, ["WU", (Zn, a, b)], [(un, o, o + CW)])

        def claims(gi):
            lo, hi = GRP[gi]
            m, q0, q1, w = (hi - lo) // 16, lo // 16, hi // 16, hi - lo
            x = str(gi)
            us, usr = T["us" + x][:, 0:w], ("us" + x, 0, w)
            Fb, Qt, JU = T["Fb" + x], T["Qt" + x], T["JU" + x]
            qt = lambda j, k=1: ("Qt" + x, j * w, (j + k) * w)
            fb = lambda j: ("Fb" + x, j * w, j * w + w)
            H = lambda nm: (nm, lo, hi)
            h = lambda nm: pf(nm, lo, hi)
            Q = lambda nm: (nm, q0, q1)
            q = lambda nm: pf(nm, q0, q1)
            cc, ccr = T.ec[:, 256 + lo:256 + hi], ("ec", 256 + lo, 256 + hi)
            qc, qcr = T.qc[:, lo:hi], ("qc", lo, hi)
            if gi in Y_TENSOR:
                S(act(h("sq"), us, F.Identity, scale=1.0 / 4096, bias=MAGIC), w, [usr], [H("sq")])
                S(act(h("qn"), h("sq"), F.Identity, scale=-4096.0, bias=4096.0 * MAGIC), w, [H("sq")], [H("qn")])
                V(tt(T.yF[:, lo:hi], h("qn"), us, A.add), w, [H("qn"), usr], [H("yF")])
                S(act(h("sq"), T.yF[:, lo:hi], F.Square, bias=T.c16[:]), w, [H("yF"), "c16"], [H("sq")])
            else:
                V(ts(h("ui"), us, 2048.0, None, A.add), w, [usr], [H("ui")])
                V(ts(h("um"), h("ui"), 4095, None, A.bitwise_and), w, [H("ui")], [H("um")])
                V(ts(T.yF[:, lo:hi], h("um"), -2048.0, None, A.add), w, [H("um")], [H("yF")])
                S(act(h("sq"), T.yF[:, lo:hi], F.Square, bias=T.c16[:]), w, [H("yF"), "c16"], [H("sq")])
            V(tt(h("tt"), h("sq"), T.ec[:, lo:hi], A.add), w, [H("sq"), H("ec")], [H("tt")])
            V(ts(h("tb"), h("tt"), 480, None, A.bitwise_and), w, [H("tt")], [H("tb")])
            V(ts(Qt[:, 5, :], h("tb"), 0.0, None, A.is_equal), w, [H("tb")], [qt(5)])
            P(mms([(qc, T.CN2[:], Qt[:, 5, :], True, True)]), w, ["CN2", qt(5)], [qcr])
            S(act(Fb[:, 0, :], qc, F.Relu, scale=-1.0, bias=-99.0), w, [qcr], [fb(0)])
            S(act(T.Fp[:, lo:hi], qc, F.Abs, bias=99.0), w, [qcr], [H("Fp")])
            S(act(Fb[:, 1, :], T.Fp[:, lo:hi], F.Relu, scale=-1.0, bias=1.0), w, [H("Fp")], [fb(1)])
            S(act(Qt[:, 6, :], T.yF[:, lo:hi], F.Copy, scale=T.row0[:]), w, [H("yF"), "row0"], [qt(6)])
            V(tt(Qt[:, 2, :], Fb[:, 0, :], cc, A.mult), w, [fb(0), ccr], [qt(2)])
            S(act(Qt[:, 0:2, :], Fb[:], F.Copy, scale=T.kcol[:]), 2 * w, ["Fb" + x, "kcol"], [qt(0, 2)])
            V(tt(Qt[:, 3, :], Fb[:, 1, :], cc, A.mult), w, [fb(1), ccr], [qt(3)])
            V(tt(Qt[:, 4, :], Fb[:, 0, :], T.yF[:, lo:hi], A.mult), 2 * w, [fb(0), H("yF")], [qt(4)])
            V(tt(h("FU"), Fb[:, 0, :], us, A.mult), w, [fb(0), usr], [H("FU")])
            P(mms([(T.kr[:, lo:hi], T.BM[:], Qt[:, 2, :], True, False), (T.kr[:, lo:hi], T.BM10[:], Fb[:, 0, :], False, False),
                   (T.kr[:, lo:hi], T.BM8[:], Fb[:, 0, :], False, False), (T.kr[:, lo:hi], T.Id[:], T.kr5[:, lo:hi], False, True)]), 4 * w,
              [qt(2), fb(0), "BM", "BM10", "BM8", "Id", "kr5"], [H("kr")])
            lc = [(T.L[:, 0:7, q0:q1], T.LR[:, r, :, :], Qt[:, :, r::16], r == 0, False) for r in range(16)]
            lc.append((T.L[:, 0:2, q0:q1], T.Id[:], T.Jc[:, :, q0:q1], False, True))
            P(mms(lc), 16 * max(64, 7 * m) + 64, ["LR", "Qt" + x, "Id", "Jc"], [("L", 0, 112)])
            V(ts(q("hm"), T.L[:, 5, q0:q1], 1.0, 10240.0, A.is_ge, A.mult), m, [("L", 80, 96)], [Q("hm")])
            V(tt(q("cand"), T.L[:, 2, q0:q1], q("hm"), A.add), m, [("L", 32, 48), Q("hm")], [Q("cand")])
            V(tt(q("kb"), q("KC"), q("cand"), A.subtract), m, ["KC", Q("cand")], [Q("kb")])
            V(ts(q("c1U"), T.L[:, 2, q0:q1], 2048.0, None, A.add), m, [("L", 32, 48)], [Q("c1U")])
            V(cp(JU[:], T.L[:, 0:2, q0:q1]), 2 * m, [("L", 0, 32)], ["JU" + x])
            for j in range(q0, q1):
                ch = j // 4
                ww = CW * (ch + 1)
                o = OFF[ch] + (j % 4) * ww
                S(act(T.AD[:, o:o + ww], T.kr[:, 0:ww], F.Abs, bias=pf("kb", j, j + 1)), ww, [("kr", 0, ww), ("kb", j, j + 1)], [("AD", o, o + ww)])
            a, b = OFF[q0 // 4], (OFF[q1 // 4] if q1 < 16 else 2560)
            V(lambda e: e.tensor_tensor_scan(T.SC[:, a:b], T.RS[:, a:b], T.AD[:, a:b], 1048576.0, A.add, A.min), (b - a) // 2, [("RS", a, b), ("AD", a, b)], [("SC", a, b)])
            for ch in range(q0 // 4, q1 // 4):
                ww, o = CW * (ch + 1), OFF[ch]
                V(ts(pf("nw", 4 * ch, 4 * ch + 4), T.SC[:, o + ww - 1:o + 4 * ww:ww], 0.25, None, A.is_lt), 4, [("SC", o, o + 4 * ww)], [("nw", 4 * ch, 4 * ch + 4)])
            V(tt(q("ndv"), q("nw"), q("Dc"), A.mult), m, [Q("nw"), "Dc"], [Q("ndv")])
            V(tt(q("pm"), q("ndv"), q("cand"), A.max), m, [Q("ndv"), Q("cand")], [Q("pm")])
            V(ts(q("posU"), q("pm"), -8192.0, None, A.add), m, [Q("pm")], [Q("posU")])
            V(tt(h("nc"), swin.indirect(q("c1U")), h("FU"), A.add), GA * w + 64, [SW, Q("c1U"), H("FU")], [H("nc")])
            V(ts(h("nd"), h("nc"), 4095, None, A.bitwise_and), w, [H("nc")], [H("nd")])
            S(act(z1[:, lo:hi], D[:].indirect(JU[:, 0, :]), F.Abs), GA * w, [Dn, "JU" + x], [(z1n, lo, hi)])
            S(act(T.z2[:, lo:hi], D[:].indirect(JU[:, 1, :]), F.Abs), GA * w, [Dn, "JU" + x], [H("z2")])

        for ch in range(4):
            cls[0] = "k%d" % ch
            chunk(ch)
        for gi in range(len(GRP)):
            cls[0] = "c%d" % gi
            claims(gi)
        for gi, (lo, hi) in enumerate(GRP):
            cls[0] = "c%d" % gi
            V(cp(T.Sw[:].indirect(pf("posU", lo // 16, hi // 16)), pf("nd", lo, hi)), SCT * (hi - lo), [("nd", lo, hi), ("posU", lo // 16, hi // 16)], ["Sw"])
        cls[0] = "y"
        LL = lambda j: ("L", 16 * j, 16 * j + 16)
        S(act(T.jk[:], T.L[:, 5, :], F.Sign, bias=-1.5, accum_out=T.acc[:]), 200, [LL(5)], ["jk", "acc"])
        V(ts(pf("hm2"), T.L[:, 5, :], 2.0, 6144.0, A.is_ge, A.mult), 16, [LL(5)], ["hm2"])
        V(tt(T["snd" + n][:], T.L[:, 3, :], pf("hm2"), A.add), 16, [LL(3), "hm2"], ["snd" + n])
        dst = T.cores[(rank + 1 + t % (len(T.cores) - 1)) % len(T.cores)]
        rid, pid = topo.addr(dst)[0], topo.addr(dst)[1]
        eng = topo.engines(core, dst)[:8]
        mask = sum(1 << e for e in eng)
        add("G", lambda e: e.remote_dma(T["rcv" + n][:], T["snd" + n][:], T.sem["an" + n], T.sem["ln" + n], pid, rid, mask), 1.0,
            ["snd" + n], [], "send", "an" + n, len(eng))
        add("N", None, EST["net"], ["snd" + n], ["rcv" + n], "recv", "an" + n, len(eng))
        V(tt(pf("n0i"), T.L[:, 6, :], pf("s5"), A.add), 16, [LL(6), "s5"], ["n0i"])
        V(ts(pf("n0"), pf("n0i"), 4095, None, A.bitwise_and), 16, ["n0i"], ["n0"])
        V(tt(pf("m0"), pf("n0"), pf("cand"), A.max), 16, ["n0", "cand"], ["m0"])
        V(ts(pf("yi"), T.L[:, 4, :], 4.0, None, A.mult), 16, [LL(4)], ["yi"])
        V(ts(pf("y7"), pf("yi"), 28, None, A.bitwise_and), 16, ["yi"], ["y7"])
        V(tt(pf("w1"), pf("hm"), pf("I32"), A.add), 16, ["hm", "I32"], ["w1"])
        V(tt(pf("w2"), pf("w1"), pf("y7"), A.add), 16, ["w1", "y7"], ["w2"])
        V(ts(pf("WLU"), pf("w2"), 0.25, None, A.mult), 16, ["w2"], ["WLU"])
        V(cp(T.XX[:].indirect(pf("WLU")), z1[:]), SCT * 256, ["WLU", z1n], ["XX"])
        xr = ("XX", XR, XR + 2048)
        if t + 1 < STEPS:
            dma("Y", T.XX[:, XD:XD + 2048], T.XX[:, XR:XR + 2048], 3.0, [xr], [("XX", XD, XD + 2048)])
            P(mms([(T.L[:, 8, 0:1], T.half[:], T.acc[:], True, True)]), 256, ["half", "acc"], [("L", 128, 129)])
        else:
            dma("Y", T.yv[:], T.XX[:, XR:XR + 2048], 3.0, [xr], [])
        sN = "sL%d" % (t + 1)
        V(tt(pf("m1"), pf("m0"), T["rcv" + n][:], A.max), 16, ["m0", "rcv" + n], ["m1"])
        V(ts(pf(sN), pf("m1"), 4095, None, A.bitwise_and), 16, ["m1"], [sN])
        if t + 1 < STEPS:
            V(cp(pf("sU%d" % (t + 1)), pf(sN)), 16, [sN], ["sU%d" % (t + 1)])
        else:
            V(cp(T.yso[:], pf(sN)), 16, [sN], ["yso"])
            dma("Y", T.ys[:], T.yso[:], 2.0, ["yso"], [])
        yr = ("qc", 256, 512)
        P(mms([(T.qc[:, 256:512], T.Id[:], T.z2[:], True, False), (T.qc[:, 256:512], T.IdN[:], XC[:, 0:256], False, True)]), 512,
          ["Id", "IdN", "z2", (XCn, 0, 256)], [yr])
        S(act(T["Y" + n][:], T.qc[:, 256:512], F.Abs), 256, [yr], ["Y" + n])
        add("G", lambda e: e.remote_dma(XC[:, XCY:XCY + 256], T["Y" + n][:], T.sem["ax" + n], T.sem["lx" + n], pid, rid, mask), 1.0,
            ["Y" + n], [], "send", "ax" + n, len(eng))
        add("N", None, EST["net"], ["Y" + n], [(XCn, XCY, XCY + 256)], "recv", "ax" + n, len(eng))
        P(mms([(T.kr[:, 256:512], T.Id[:], z1[:], True, False), (T.kr[:, 256:512], T.Id[:], XC[:, 0:256], False, False),
               (T.kr[:, 256:512], T.Id[:], T.mhalf[:], False, True)]), 768, ["Id", z1n, (XCn, 0, 256), "mhalf"], [("kr", 256, 512)])
        S(act(pf("ha"), T.kr[:, 256:512], F.Identity, bias=MAGIC, scale=0.5), 256, [("kr", 256, 512)], ["ha"])
        S(act(XC[:, XCH:XCH + 256], pf("ha"), F.Identity, bias=-MAGIC), 256, ["ha"], [(XCn, XCH, XCH + 256)])
        V(ts(pf("cm"), T["rcv" + n][:], 4096.0, None, A.min), 16, ["rcv" + n], ["cm"])
        V(tt(pf("xm"), pf("cm"), pf("hm"), A.max), 16, ["cm", "hm"], ["xm"])
        V(tt(pf("xi"), pf("xm"), pf("I16"), A.add), 16, ["xm", "I16"], ["xi"])
        V(ts(pf("XLU"), pf("xi"), 0.0625, None, A.mult), 16, ["xi"], ["XLU"])
        nx = "XC%d" % (t + 1)
        S(act(T[nx][:, 0:256], XC[:].indirect(pf("XLU")), F.Copy), GA * 256, [XCn, "XLU"], [(nx, 0, 256)])
        if t + 1 == STEPS:
            dma("Y", T.yx[:], T[nx][:, 0:256], 2.0, [(nx, 0, 256)], [])

    for t in range(STEPS):
        step(t)

    for j in range(0, 16, 2):
        a = 256 * j
        r, w = [("Sw", a, a + 512)], [("S16", a, a + 512)]
        if j % 4 == 0:
            V(ts(T.S16[:, a:a + 512], T.Sw[:, a:a + 512], -2048.0, None, A.add), 512, r, w)
        else:
            S(act(T.S16[:, a:a + 512], T.Sw[:, a:a + 512], F.Identity, bias=-2048.0), 512, r, w)
        P(mms([(T.ab0[:, 0:256], T.Id[:], T.S16[:, 256 * k:256 * k + 256], k == 0, k == 15) for k in (j, j + 1)]), 512,
          ["Id", ("S16", a, a + 512), ("ab0", 0, 256)], [("ab0", 0, 256)])
    V(ts(pf("yto"), T.ab0[:, 0:256], 32768.0, None, A.add), 256, [("ab0", 0, 256)], ["yto"])
    dma("Y", T.yt[:], pf("yto"), 2.0, ["yto"], [])


def depends(ops):
    seen = {}
    for i, o in enumerate(ops):
        d = set()
        acc = [(x, False) for x in o["r"]] + [(x, True) for x in o["w"]]
        for (b, lo, hi), wr in acc:
            for (j, l2, h2, w2) in seen.get(b, ()):
                if (wr or w2) and lo < h2 and l2 < hi:
                    d.add(j)
                elif b in PSUMS and ops[j]["q"] != o["q"]:
                    d.add(j)
        for (b, lo, hi), wr in acc:
            lst = seen.setdefault(b, [])
            if wr and b not in PSUMS:
                lst[:] = [x for x in lst if not (lo <= x[1] and x[2] <= hi)]
            lst.append((i, lo, hi, wr))
            if b in PSUMS and len(lst) > 60:
                del lst[:len(lst) - 60]
        d.discard(i)
        o["d"] = sorted(d)


def schedule(ops):
    wake = EST["wake"]
    n = len(ops)
    succ = [[] for _ in range(n)]
    need = [0] * n
    for i, o in enumerate(ops):
        for j in o["d"]:
            succ[j].append(i)
        need[i] = len(o["d"])
    prio = [0.0] * n
    for i in range(n - 1, -1, -1):
        best = 0.0
        for k in succ[i]:
            best = max(best, prio[k] + wake)
        prio[i] = best + ops[i]["dur"]
    for i in range(n):
        prio[i] += BOOST.get(ops[i]["cls"], 0.0)
    free = {}
    ready = [(0.0, i) for i in range(n) if need[i] == 0]
    end = [0.0] * n
    at = [0.0] * n
    order = []
    while ready:
        cand = [(max(r, free.get(ops[i]["q"], 0.0)), -prio[i], i) for r, i in ready]
        s0 = min(cand)[0]
        s, _, i = min([c for c in cand if c[0] <= s0 + LOOK], key=lambda c: c[1])
        ready = [x for x in ready if x[1] != i]
        o = ops[i]
        end[i] = s + o["dur"]
        at[i] = s
        if o["kind"] == "dma":
            free[o["q"]] = s + 0.1
        elif o["kind"] != "recv":
            free[o["q"]] = end[i]
        order.append(i)
        for k in succ[i]:
            need[k] -= 1
            if need[k] == 0:
                ready.append((max([end[j] + wake for j in ops[k]["d"]]), k))
    return order, max(end), at, end


def rank_program(g, core, T, topo):
    if T.rank_of(core) is None:
        return
    ops = []
    build(core, T, topo, ops)
    depends(ops)
    order = schedule(ops)[0]
    eng = {"V": g.vector, "S": g.scalar, "P": g.tensor, "G": g, "Y": g.sync}
    know = {}
    for q in eng:
        know[q] = {}
    count = {}
    token = {}
    clock = {}

    def learn(q, tok):
        k = know[q]
        for s, c in clock.get(tok, {}).items():
            if k.get(s, 0) < c:
                k[s] = c
        if k.get(tok[0], 0) < tok[1]:
            k[tok[0]] = tok[1]

    for i in order:
        o = ops[i]
        if o["kind"] == "recv":
            token[i] = (o["sem"], o["cnt"])
            continue
        q = o["q"]
        e = eng[q]
        want = {}
        for j in o["d"]:
            if ops[j]["kind"] == "send":
                continue
            s, c = token[j]
            want[s] = max(want.get(s, 0), c)
        for s in sorted(want, key=lambda s: -sum(clock.get((s, want[s]), {}).values())):
            if know[q].get(s, 0) < want[s]:
                e.wait_ge(T.sem[s], want[s])
                learn(q, (s, want[s]))
        ins = o["fn"](e)
        if o["kind"] == "send":
            continue
        if o["kind"] == "dma":
            ins.then_inc(T.sem[o["sem"]], 16)
            token[i] = (o["sem"], 16)
        else:
            s = "e" + q
            count[s] = count.get(s, 0) + 1
            ins.then_inc(T.sem[s], 1)
            token[i] = (s, count[s])
        clock[token[i]] = dict(know[q])
        clock[token[i]][token[i][0]] = token[i][1]
    for s in sorted(count):
        g.wait_ge(T.sem[s], count[s])
    for o in ops:
        if o["kind"] == "dma":
            g.wait_ge(T.sem[o["sem"]], 16)
        if o["kind"] == "send":
            g.wait_ge(T.sem["l" + o["sem"][1:]], o["cnt"])
            g.wait_ge(T.sem[o["sem"]], o["cnt"])
